import numpy as np
import ml_dtypes


def mxq(x, axis, fmt="e4m3"):
    dtype, down = {"e4m3": (ml_dtypes.float8_e4m3fn, 7), "e5m2": (ml_dtypes.float8_e5m2, 14)}[fmt]
    v = np.moveaxis(np.asarray(x, np.float32).astype(ml_dtypes.bfloat16).astype(np.float64), axis, -1)
    blocks = v.reshape(v.shape[:-1] + (-1, 32))
    amax = np.abs(blocks).max(-1, keepdims=True)
    byte = np.maximum(np.where(amax > 0, np.frexp(amax)[1] - 1 + 127, 0) - down, 1)
    scale = np.exp2(byte - 127.0)
    codes = (blocks / scale).astype(np.float32).astype(dtype).astype(np.float64)
    return np.moveaxis((codes * scale).reshape(v.shape), -1, axis)


WIDE = False


def mx_kscale(k):
    if not WIDE:
        return np.ones(k)
    levels = np.array([10, -10, 5, -5, 0])
    if k % 512:
        return np.exp2(np.random.permutation(np.resize(levels, k // 32))).repeat(32)
    a = np.empty((k // 512, 16))
    for p in range(k // 512):
        a[p, :8] = np.random.permutation(np.resize(levels, 8))
        for g in range(8):
            far = levels[np.abs(levels - a[p, g]) >= 10]
            a[p, g + 8] = far[np.random.randint(len(far))]
    return np.exp2(a.ravel()).repeat(32)


def f64(x):
    return np.asarray(x).astype(np.float64)


def striped(idx):
    return np.tile(idx.reshape(-1, 16).T, (8, 1)).astype(np.uint16)


def unstriped(offs):
    return offs[:16].T.reshape(-1).astype(np.int64)


E2M1 = np.array([0.0, 0.5, 1.0, 1.5, 2.0, 3.0, 4.0, 6.0, -0.0, -0.5, -1.0, -1.5, -2.0, -3.0, -4.0, -6.0])


def pack_weight(w, fmt):
    k, n = w.shape
    w = f64(np.asarray(w, np.float32).astype(ml_dtypes.bfloat16)).reshape(k // 32, 32, n)
    amax = np.abs(w).max(1)
    if fmt == "e4m3":
        byte = np.frexp(amax)[1] - 1 + 127 - 7
    else:
        mant, ex = np.frexp(amax / 6.0)
        byte = np.where(mant > 0.5, ex, ex - 1) + 127
    byte = np.clip(np.where(amax > 0, byte, 1), 1, 254)
    scaled = (w * np.exp2(127.0 - byte)[:, None, :]).reshape(k, n).astype(np.float32)
    by_word = np.ascontiguousarray(scaled.reshape(k // 512, 128, 4, n).transpose(0, 1, 3, 2))
    if fmt == "e4m3":
        words = by_word.astype(ml_dtypes.float8_e4m3fn).view(np.uint8)
    else:
        c = by_word.astype(ml_dtypes.float4_e2m1fn).view(np.uint8) & 0xF
        words = (c[..., 0::2] | (c[..., 1::2] << 4)).reshape(k // 512, 128, 2 * n)
    return np.ascontiguousarray(words), np.ascontiguousarray(byte.astype(np.uint8).reshape(k // 512, 16, n))


def unpack_weight(words, scales, fmt):
    g, _, n = scales.shape
    words = np.ascontiguousarray(words).reshape(g, 128, n, -1)
    if fmt == "e4m3":
        vals = words.view(ml_dtypes.float8_e4m3fn).astype(np.float64)
    else:
        nib = np.empty((g, 128, n, 4), np.uint8)
        nib[..., 0::2] = words & 0xF
        nib[..., 1::2] = words >> 4
        vals = E2M1[nib]
    vals = vals * np.repeat(np.exp2(scales.astype(np.float64) - 127.0), 8, axis=1)[..., None]
    return vals.transpose(0, 1, 3, 2).reshape(g * 512, n)


def relu2(v):
    return np.maximum(v, 0.0) ** 2


K, T, E, C, N = 1024, 1024, 8, 256, 512
R = 8


def by_expert(wq, xq):
    return np.concatenate([wq[e].T @ xq[:, e * C:(e + 1) * C] for e in range(E)], axis=1)


def setup_inputs():
    n = np.random.standard_normal
    s = mx_kscale(K)[:, None]
    slot_token = np.concatenate([r * (T // R) + np.random.permutation(T // R)[:C // R] for e in range(E) for r in range(R)])
    w = [pack_weight(m, "e2m1") for m in n((E, K, N)) / np.sqrt(K) / s[None]]
    return {
        "xT": (n((K, T)) * s).astype(np.float32),
        "w_words": np.stack([m[0] for m in w]),
        "w_scales": np.stack([m[1] for m in w]),
        "b": (0.3 * n((N, E))).astype(np.float32),
        "offs": striped(slot_token),
    }


def reference(xT, w_words, w_scales, b, offs):
    idx = unstriped(offs)
    w = np.stack([unpack_weight(w_words[e], w_scales[e], "e2m1") for e in range(E)])
    xq = mxq(f64(xT)[:, idx], 0, "e4m3")
    y = by_expert(w, xq)
    y = relu2(y + np.repeat(f64(b), C, axis=1))
    return y.reshape(N, E, R, C // R).transpose(0, 2, 1, 3).reshape(N, E * C)

@@ -1,0 +1,160 @@
+from contextlib import ExitStack
+
+import concourse.mybir as mybir
+
+K, T, E, C, N, R = 1024, 1024, 8, 256, 512, 8
+U = C // R
+P = 128
+FLOPS = 2 * E * C * K * N
+
+F32 = mybir.dt.float32
+BF16 = mybir.dt.bfloat16
+I32 = mybir.dt.int32
+U32 = mybir.dt.uint32
+U16 = mybir.dt.uint16
+U8 = mybir.dt.uint8
+FP8X4 = mybir.dt.float8_e4m3fn_x4
+FP4X4 = mybir.dt.float4_e2m1fn_x4
+RELU = mybir.ActivationFunctionType.Relu
+SQUARE = mybir.ActivationFunctionType.Square
+MULT = mybir.AluOpType.mult
+ADD = mybir.AluOpType.add
+MAX = mybir.AluOpType.max
+
+
+def tile_moe_eps_lin_relu2_kernel(tc, xT, w_words, w_scales, b, offs, out):
+    nc = tc.nc
+    with ExitStack() as ctx:
+        keep = ctx.enter_context(tc.tile_pool(name="keep", bufs=1))
+        psum = ctx.enter_context(tc.psum_pool(name="psum", bufs=8))
+
+        offsets = keep.tile([P, E * C // 16], U16, name="offsets")
+        raw = [[keep.tile([P, 4, 512], F32, name=f"raw{a}{c}") for c in range(2)] for a in range(2)]
+        grouped = [[keep.tile([P, 512, 4], BF16, align_bytes=64, name=f"grouped{a}{c}") for c in range(2)] for a in range(2)]
+        words = [keep.tile([P, T], U32, align_bytes=64, name=f"words{a}") for a in range(2)]
+        scales = keep.tile([P, T], U8, align_bytes=64, name="scales")
+        slot_words = [keep.tile([P, E * C], U32, align_bytes=64, name=f"slot_words{a}") for a in range(2)]
+        slot_scales = [keep.tile([P, E * C], U8, align_bytes=64, name=f"slot_scales{a}") for a in range(2)]
+        ww = keep.tile([P, E * 2, 2 * N], U8, align_bytes=64, name="ww")
+        ws = keep.tile([P, E * 2, N], U8, align_bytes=64, name="ws")
+        bias = keep.tile([P, N // P, E], F32, name="bias")
+        groups = [[0, 1, 2, 3], [4, 5, 6, 7]]
+        results = [keep.tile([P, N // P, R, len(g), U], F32, name=f"results{g[0]}") for g in groups]
+
+        def load_x(a, c):
+            rows = xT[512 * a : 512 * (a + 1), 512 * c : 512 * (c + 1)]
+            nc.sync.dma_start(raw[a][c][:], rows.rearrange("(p j) w -> p j w", j=4))
+
+        nc.gpsimd.memset(scales[:], 0)
+        nc.gpsimd.memset(ws[:].bitcast(I32), 0)
+        nc.gpsimd.memset(slot_scales[1][:].bitcast(I32), 0)
+
+        load_x(0, 0)
+        load_x(0, 1)
+        nc.sync.dma_start(offsets[:], offs)
+        load_x(1, 0)
+        load_x(1, 1)
+        nc.scalar.dma_start(bias[:], b.rearrange("(t p) e -> p t e", p=P))
+        scale_rows = w_scales.bitcast(I32).rearrange("e a q n -> q (e a) n")
+        for q in range(4):
+            nc.sync.dma_start(ws[32 * q : 32 * q + 4, :, :].bitcast(I32), scale_rows[4 * q : 4 * q + 4])
+        word_rows = w_words.bitcast(I32).rearrange("e a p n -> p (e a) n")
+        for h in range(2):
+            nc.sync.dma_start(ww[:, 8 * h : 8 * h + 8, :].bitcast(I32), word_rows[:, 8 * h : 8 * h + 8, :])
+
+        def interleave(copy, a, c, lo, hi):
+            copy(
+                out=grouped[a][c][:, lo:hi, :].rearrange("p (g i) j -> p g j i", i=4),
+                in_=raw[a][c][:, :, lo:hi].rearrange("p j (g i) -> p g j i", i=4),
+            )
+
+        def quantize(a, c):
+            cols = slice(512 * c, 512 * (c + 1))
+            nc.vector.quantize_mx(
+                out=words[a][:, cols].bitcast(FP8X4),
+                scales=scales[4 * a : P, cols],
+                in_=grouped[a][c][:].rearrange("p w j -> p (w j)"),
+            )
+
+        def gather_words(a, lo, hi):
+            nc.vector.tensor_copy(slot_words[a][:, lo:hi], words[a][:].indirect(offsets[:, lo // 16 : hi // 16]))
+
+        def gather_scales(lo, hi):
+            nc.vector.tensor_copy(slot_scales[0][:, lo:hi], scales[:].indirect(offsets[:, lo // 16 : hi // 16]))
+            for q in range(4):
+                nc.sync.dma_start(
+                    slot_scales[1][32 * q : 32 * q + 4, lo:hi].bitcast(I32),
+                    slot_scales[0][32 * q + 4 : 32 * q + 8, lo:hi].bitcast(I32),
+                )
+
+        def multiply(e0, t):
+            bank = psum.tile([P, 2, C], F32, name="bank")
+            for i in range(2):
+                e = e0 + i
+                for h in range(2):
+                    cols = slice(C * e + P * h, C * e + P * (h + 1))
+                    for a in range(2):
+                        nc.tensor.matmul_mx(
+                            out=bank[:, i, P * h : P * (h + 1)],
+                            lhsT=ww[:, 2 * e + a, 2 * P * t : 2 * P * (t + 1)].bitcast(FP4X4),
+                            lhsT_scale=ws[:, 2 * e + a, P * t : P * (t + 1)],
+                            rhs=slot_words[a][:, cols].bitcast(FP8X4),
+                            rhs_scale=slot_scales[a][:, cols],
+                            start=(a == 0),
+                            stop=(a == 1),
+                        )
+            return bank
+
+        def relu(engine, bank, e, t):
+            g, place = e // 4, e % 4
+            sums = bank[:, e % 2, :].rearrange("p (m u) -> p m u", u=U)
+            if engine == "s":
+                nc.scalar.activation(results[g][:, t, :, place, :], sums, RELU, bias=bias[:, t, e : e + 1])
+            else:
+                nc.vector.tensor_scalar(results[g][:, t, :, place, :], sums, bias[:, t, e : e + 1], 0.0, ADD, MAX)
+
+        def square(engine, g, t, half):
+            v = results[g][:, t, 4 * half : 4 * half + 4].rearrange("p m e u -> p (m e u)")
+            if engine == "s":
+                nc.scalar.activation(v, v, SQUARE)
+            elif engine == "v":
+                nc.vector.tensor_tensor(v, v, v, MULT)
+            else:
+                nc.gpsimd.tensor_tensor(v, v, v, MULT)
+
+        def store(g, t):
+            rows = out[P * t : P * (t + 1), :].rearrange("p (m e u) -> p m e u", m=R, e=E)
+            nc.sync.dma_start(rows[:, :, 4 * g : 4 * g + 4, :], results[g][:, t])
+
+        for c in range(2):
+            interleave(nc.vector.tensor_copy, 0, c, 0, 384)
+            interleave(nc.scalar.copy, 0, c, 384, 512)
+            quantize(0, c)
+        interleave(nc.scalar.copy, 1, 0, 0, 512)
+        interleave(nc.scalar.copy, 1, 1, 192, 512)
+        interleave(nc.vector.tensor_copy, 1, 1, 0, 192)
+        gather_words(0, 0, 512)
+        gather_words(0, 512, 1024)
+        quantize(1, 0)
+        quantize(1, 1)
+        gather_scales(0, 512)
+        gather_scales(512, 1024)
+        gather_words(1, 0, 512)
+        gather_words(1, 512, 1024)
+        gather_words(0, 1024, 1536)
+        gather_words(0, 1536, 2048)
+        gather_scales(1024, 1536)
+        gather_scales(1536, 2048)
+        gather_words(1, 1024, 1536)
+        gather_words(1, 1536, 2048)
+        relu_engine = ["s","s","s","s","s","s","v","v"]
+        square_engine = ["gs","sv"]
+        for g in range(2):
+            for t in range(4):
+                for e in (4 * g, 4 * g + 2):
+                    bank = multiply(e, t)
+                    relu(relu_engine[e], bank, e, t)
+                    relu(relu_engine[e + 1], bank, e + 1, t)
+                square(square_engine[g][0], g, t, 0)
+                square(square_engine[g][1], g, t, 1)
+                store(g, t)

@@ -38,8 +38,7 @@ def tile_moe_eps_lin_relu2_kernel(tc, xT, w_words, w_scales, b, offs, out):
         ww = keep.tile([P, E * 2, 2 * N], U8, align_bytes=64, name="ww")
         ws = keep.tile([P, E * 2, N], U8, align_bytes=64, name="ws")
         bias = keep.tile([P, N // P, E], F32, name="bias")
-        groups = [[0, 1, 2, 3], [4, 5, 6, 7]]
-        results = [keep.tile([P, N // P, R, len(g), U], F32, name=f"results{g[0]}") for g in groups]
+        results = [keep.tile([P, R, E, U], F32, name=f"results{t}") for t in range(4)]
 
         def load_x(a, c):
             rows = xT[512 * a : 512 * (a + 1), 512 * c : 512 * (c + 1)]
@@ -106,33 +105,31 @@ def tile_moe_eps_lin_relu2_kernel(tc, xT, w_words, w_scales, b, offs, out):
             return bank
 
         def relu(engine, bank, e, t):
-            g, place = e // 4, e % 4
             sums = bank[:, e % 2, :].rearrange("p (m u) -> p m u", u=U)
             if engine == "s":
-                nc.scalar.activation(results[g][:, t, :, place, :], sums, RELU, bias=bias[:, t, e : e + 1])
+                nc.scalar.activation(results[t][:, :, e, :], sums, RELU, bias=bias[:, t, e : e + 1])
             else:
-                nc.vector.tensor_scalar(results[g][:, t, :, place, :], sums, bias[:, t, e : e + 1], 0.0, ADD, MAX)
+                nc.vector.tensor_scalar(results[t][:, :, e, :], sums, bias[:, t, e : e + 1], 0.0, ADD, MAX)
 
         def square(engine, g, t, half):
-            v = results[g][:, t, 4 * half : 4 * half + 4].rearrange("p m e u -> p (m e u)")
+            v = results[t][:, 4 * half : 4 * half + 4, 4 * g : 4 * g + 4, :].rearrange("p m e u -> p m (e u)")
             if engine == "s":
                 nc.scalar.activation(v, v, SQUARE)
-            elif engine == "v":
-                nc.vector.tensor_tensor(v, v, v, MULT)
             else:
-                nc.gpsimd.tensor_tensor(v, v, v, MULT)
+                nc.vector.tensor_tensor(v, v, v, MULT)
 
-        def store(g, t):
+        def store(t, half, lo, hi):
+            ranks = slice(4 * half, 4 * half + 4)
             rows = out[P * t : P * (t + 1), :].rearrange("p (m e u) -> p m e u", m=R, e=E)
-            nc.sync.dma_start(rows[:, :, 4 * g : 4 * g + 4, :], results[g][:, t])
+            nc.sync.dma_start(rows[:, ranks, lo:hi, :], results[t][:, ranks, lo:hi, :])
 
         for c in range(2):
             interleave(nc.vector.tensor_copy, 0, c, 0, 384)
             interleave(nc.scalar.copy, 0, c, 384, 512)
             quantize(0, c)
         interleave(nc.scalar.copy, 1, 0, 0, 512)
-        interleave(nc.scalar.copy, 1, 1, 192, 512)
-        interleave(nc.vector.tensor_copy, 1, 1, 0, 192)
+        interleave(nc.scalar.copy, 1, 1, 128, 512)
+        interleave(nc.vector.tensor_copy, 1, 1, 0, 128)
         gather_words(0, 0, 512)
         gather_words(0, 512, 1024)
         quantize(1, 0)
@@ -147,14 +144,16 @@ def tile_moe_eps_lin_relu2_kernel(tc, xT, w_words, w_scales, b, offs, out):
         gather_scales(1536, 2048)
         gather_words(1, 1024, 1536)
         gather_words(1, 1536, 2048)
-        relu_engine = ["s","s","s","s","s","s","v","v"]
-        square_engine = ["gs","sv"]
-        for g in range(2):
-            for t in range(4):
+        for g, order in enumerate(((0, 1, 2, 3), (3, 0, 1, 2))):
+            for t in order:
                 for e in (4 * g, 4 * g + 2):
                     bank = multiply(e, t)
-                    relu(relu_engine[e], bank, e, t)
-                    relu(relu_engine[e + 1], bank, e + 1, t)
-                square(square_engine[g][0], g, t, 0)
-                square(square_engine[g][1], g, t, 1)
-                store(g, t)
+                    engine = "s" if e == 0 or (e == 2 and t < 2) else "v"
+                    relu(engine, bank, e, t)
+                    relu(engine, bank, e + 1, t)
+                for half in range(2):
+                    square("s" if g == 0 or t < 2 else "v", g, t, half)
+                    if t < 3:
+                        store(t, half, 4 * g, 4 * g + 4)
+                    elif g == 1:
+                        store(t, half, 0, E)

@@ -54,9 +54,9 @@ def tile_moe_eps_lin_relu2_kernel(tc, xT, w_words, w_scales, b, offs, out):
         load_x(1, 0)
         load_x(1, 1)
         nc.scalar.dma_start(bias[:], b.rearrange("(t p) e -> p t e", p=P))
-        scale_rows = w_scales.bitcast(I32).rearrange("e a q n -> q (e a) n")
-        for q in range(4):
-            nc.sync.dma_start(ws[32 * q : 32 * q + 4, :, :].bitcast(I32), scale_rows[4 * q : 4 * q + 4])
+        scale_rows = w_scales.bitcast(I32).rearrange("e a (q r) n -> r q (e a) n", r=4)
+        for r in range(4):
+            nc.sync.dma_start(ws[r:P:32, :, :].bitcast(I32), scale_rows[r])
         word_rows = w_words.bitcast(I32).rearrange("e a p n -> p (e a) n")
         for h in range(2):
             nc.sync.dma_start(ww[:, 8 * h : 8 * h + 8, :].bitcast(I32), word_rows[:, 8 * h : 8 * h + 8, :])
@@ -80,11 +80,9 @@ def tile_moe_eps_lin_relu2_kernel(tc, xT, w_words, w_scales, b, offs, out):
 
         def gather_scales(lo, hi):
             nc.vector.tensor_copy(slot_scales[0][:, lo:hi], scales[:].indirect(offsets[:, lo // 16 : hi // 16]))
-            for q in range(4):
-                nc.sync.dma_start(
-                    slot_scales[1][32 * q : 32 * q + 4, lo:hi].bitcast(I32),
-                    slot_scales[0][32 * q + 4 : 32 * q + 8, lo:hi].bitcast(I32),
-                )
+
+        def move_scales(queue, lo, hi):
+            queue.dma_start(slot_scales[1][: P - 4, lo:hi].bitcast(I32), slot_scales[0][4:P, lo:hi].bitcast(I32))
 
         def multiply(e0, t):
             bank = psum.tile([P, 2, C], F32, name="bank")
@@ -111,17 +109,16 @@ def tile_moe_eps_lin_relu2_kernel(tc, xT, w_words, w_scales, b, offs, out):
             else:
                 nc.vector.tensor_scalar(results[t][:, :, e, :], sums, bias[:, t, e : e + 1], 0.0, ADD, MAX)
 
-        def square(engine, g, t, half):
-            v = results[t][:, 4 * half : 4 * half + 4, 4 * g : 4 * g + 4, :].rearrange("p m e u -> p m (e u)")
+        def square(engine, g, t):
+            v = results[t][:, :, 4 * g : 4 * g + 4, :].rearrange("p m e u -> p m (e u)")
             if engine == "s":
                 nc.scalar.activation(v, v, SQUARE)
             else:
                 nc.vector.tensor_tensor(v, v, v, MULT)
 
-        def store(t, half, lo, hi):
-            ranks = slice(4 * half, 4 * half + 4)
+        def store(t, lo, hi):
             rows = out[P * t : P * (t + 1), :].rearrange("p (m e u) -> p m e u", m=R, e=E)
-            nc.sync.dma_start(rows[:, ranks, lo:hi, :], results[t][:, ranks, lo:hi, :])
+            nc.sync.dma_start(rows[:, :, lo:hi, :], results[t][:, :, lo:hi, :])
 
         for c in range(2):
             interleave(nc.vector.tensor_copy, 0, c, 0, 384)
@@ -135,13 +132,28 @@ def tile_moe_eps_lin_relu2_kernel(tc, xT, w_words, w_scales, b, offs, out):
         quantize(1, 0)
         quantize(1, 1)
         gather_scales(0, 512)
+        move_scales(nc.sync, 0, 512)
         gather_scales(512, 1024)
+        move_scales(nc.sync, 512, 1024)
+        warm = psum.tile([P, 2, C], F32, name="bank")
+        for i in range(12):
+            nc.tensor.matmul_mx(
+                out=warm[:, 0, :P],
+                lhsT=ww[:, 0, : 2 * P].bitcast(FP4X4),
+                lhsT_scale=ws[:, 0, :P],
+                rhs=slot_words[0][:, :P].bitcast(FP8X4),
+                rhs_scale=slot_scales[0][:, :P],
+                start=True,
+                stop=True,
+            )
         gather_words(1, 0, 512)
         gather_words(1, 512, 1024)
         gather_words(0, 1024, 1536)
         gather_words(0, 1536, 2048)
         gather_scales(1024, 1536)
+        move_scales(nc.sync, 1024, 1536)
         gather_scales(1536, 2048)
+        move_scales(nc.sync, 1536, 2048)
         gather_words(1, 1024, 1536)
         gather_words(1, 1536, 2048)
         for g, order in enumerate(((0, 1, 2, 3), (3, 0, 1, 2))):
@@ -151,9 +163,8 @@ def tile_moe_eps_lin_relu2_kernel(tc, xT, w_words, w_scales, b, offs, out):
                     engine = "s" if e == 0 or (e == 2 and t < 2) else "v"
                     relu(engine, bank, e, t)
                     relu(engine, bank, e + 1, t)
-                for half in range(2):
-                    square("s" if g == 0 or t < 2 else "v", g, t, half)
-                    if t < 3:
-                        store(t, half, 4 * g, 4 * g + 4)
-                    elif g == 1:
-                        store(t, half, 0, E)
+                square("s" if g == 0 or t < 2 else "v", g, t)
+                if t < 3:
+                    store(t, 4 * g, 4 * g + 4)
+                elif g == 1:
+                    store(t, 0, E)

@@ -53,7 +53,7 @@ def tile_moe_eps_lin_relu2_kernel(tc, xT, w_words, w_scales, b, offs, out):
         nc.sync.dma_start(offsets[:], offs)
         load_x(1, 0)
         load_x(1, 1)
-        nc.scalar.dma_start(bias[:], b.rearrange("(t p) e -> p t e", p=P))
+        nc.sync.dma_start(bias[:], b.rearrange("(t p) e -> p t e", p=P))
         scale_rows = w_scales.bitcast(I32).rearrange("e a (q r) n -> r q (e a) n", r=4)
         for r in range(4):
             nc.sync.dma_start(ws[r:P:32, :, :].bitcast(I32), scale_rows[r])
@@ -109,16 +109,16 @@ def tile_moe_eps_lin_relu2_kernel(tc, xT, w_words, w_scales, b, offs, out):
             else:
                 nc.vector.tensor_scalar(results[t][:, :, e, :], sums, bias[:, t, e : e + 1], 0.0, ADD, MAX)
 
-        def square(engine, g, t):
-            v = results[t][:, :, 4 * g : 4 * g + 4, :].rearrange("p m e u -> p m (e u)")
+        def square(engine, g, t, ranks):
+            v = results[t][:, ranks, 4 * g : 4 * g + 4, :].rearrange("p m e u -> p m (e u)")
             if engine == "s":
                 nc.scalar.activation(v, v, SQUARE)
             else:
                 nc.vector.tensor_tensor(v, v, v, MULT)
 
-        def store(t, lo, hi):
+        def store(t, ranks, lo, hi):
             rows = out[P * t : P * (t + 1), :].rearrange("p (m e u) -> p m e u", m=R, e=E)
-            nc.sync.dma_start(rows[:, :, lo:hi, :], results[t][:, :, lo:hi, :])
+            nc.sync.dma_start(rows[:, ranks, lo:hi, :], results[t][:, ranks, lo:hi, :])
 
         for c in range(2):
             interleave(nc.vector.tensor_copy, 0, c, 0, 384)
@@ -132,9 +132,9 @@ def tile_moe_eps_lin_relu2_kernel(tc, xT, w_words, w_scales, b, offs, out):
         quantize(1, 0)
         quantize(1, 1)
         gather_scales(0, 512)
-        move_scales(nc.sync, 0, 512)
+        move_scales(nc.scalar, 0, 512)
         gather_scales(512, 1024)
-        move_scales(nc.sync, 512, 1024)
+        move_scales(nc.scalar, 512, 1024)
         warm = psum.tile([P, 2, C], F32, name="bank")
         for i in range(12):
             nc.tensor.matmul_mx(
@@ -156,15 +156,23 @@ def tile_moe_eps_lin_relu2_kernel(tc, xT, w_words, w_scales, b, offs, out):
         move_scales(nc.sync, 1536, 2048)
         gather_words(1, 1024, 1536)
         gather_words(1, 1536, 2048)
-        for g, order in enumerate(((0, 1, 2, 3), (3, 0, 1, 2))):
-            for t in order:
-                for e in (4 * g, 4 * g + 2):
-                    bank = multiply(e, t)
-                    engine = "s" if e == 0 or (e == 2 and t < 2) else "v"
-                    relu(engine, bank, e, t)
-                    relu(engine, bank, e + 1, t)
-                square("s" if g == 0 or t < 2 else "v", g, t)
+        all_ranks = slice(0, R)
+        halves = (slice(0, R // 2), slice(R // 2, R))
+        for t in range(4):
+            for e in (0, 2):
+                bank = multiply(e, t)
+                engine = "s" if e == 0 or t < 2 else "v"
+                relu(engine, bank, e, t)
+                relu(engine, bank, e + 1, t)
+            for ranks in halves if t == 0 else (all_ranks,):
+                square("s" if t < 2 else "v", 0, t, ranks)
                 if t < 3:
-                    store(t, 4 * g, 4 * g + 4)
-                elif g == 1:
-                    store(t, 0, E)
+                    store(t, ranks, 0, 4)
+        for t in (3, 0, 1, 2):
+            for e, engine in ((4, "v"), (6, "s")):
+                bank = multiply(e, t)
+                relu(engine, bank, e, t)
+                relu(engine, bank, e + 1, t)
+            for engine, ranks in zip("sv", halves):
+                square(engine, 1, t, ranks)
+                store(t, ranks, 0 if t == 3 else 4, 8)

from contextlib import ExitStack

import concourse.mybir as mybir

K, T, E, C, N, R = 1024, 1024, 8, 256, 512, 8
U = C // R
P = 128
FLOPS = 2 * E * C * K * N

F32 = mybir.dt.float32
BF16 = mybir.dt.bfloat16
I32 = mybir.dt.int32
U32 = mybir.dt.uint32
U16 = mybir.dt.uint16
U8 = mybir.dt.uint8
FP8X4 = mybir.dt.float8_e4m3fn_x4
FP4X4 = mybir.dt.float4_e2m1fn_x4
RELU = mybir.ActivationFunctionType.Relu
SQUARE = mybir.ActivationFunctionType.Square
MULT = mybir.AluOpType.mult
ADD = mybir.AluOpType.add
MAX = mybir.AluOpType.max


def tile_moe_eps_lin_relu2_kernel(tc, xT, w_words, w_scales, b, offs, out):
    nc = tc.nc
    with ExitStack() as ctx:
        keep = ctx.enter_context(tc.tile_pool(name="keep", bufs=1))
        psum = ctx.enter_context(tc.psum_pool(name="psum", bufs=8))

        offsets = keep.tile([P, E * C // 16], U16, name="offsets")
        raw = [[keep.tile([P, 4, 512], F32, name=f"raw{a}{c}") for c in range(2)] for a in range(2)]
        grouped = [[keep.tile([P, 512, 4], BF16, align_bytes=64, name=f"grouped{a}{c}") for c in range(2)] for a in range(2)]
        words = [keep.tile([P, T], U32, align_bytes=64, name=f"words{a}") for a in range(2)]
        scales = keep.tile([P, T], U8, align_bytes=64, name="scales")
        slot_words = [keep.tile([P, E * C], U32, align_bytes=64, name=f"slot_words{a}") for a in range(2)]
        slot_scales = [keep.tile([P, E * C], U8, align_bytes=64, name=f"slot_scales{a}") for a in range(2)]
        ww = keep.tile([P, E * 2, 2 * N], U8, align_bytes=64, name="ww")
        ws = keep.tile([P, E * 2, N], U8, align_bytes=64, name="ws")
        bias = keep.tile([P, N // P, E], F32, name="bias")
        results = [keep.tile([P, R, E, U], F32, name=f"results{t}") for t in range(4)]

        def load_x(a, c):
            rows = xT[512 * a : 512 * (a + 1), 512 * c : 512 * (c + 1)]
            nc.sync.dma_start(raw[a][c][:], rows.rearrange("(p j) w -> p j w", j=4))

        nc.gpsimd.memset(scales[:], 0)
        nc.gpsimd.memset(ws[:].bitcast(I32), 0)
        nc.gpsimd.memset(slot_scales[1][:].bitcast(I32), 0)

        load_x(0, 0)
        load_x(0, 1)
        nc.sync.dma_start(offsets[:], offs)
        load_x(1, 0)
        load_x(1, 1)
        nc.sync.dma_start(bias[:], b.rearrange("(t p) e -> p t e", p=P))
        scale_rows = w_scales.bitcast(I32).rearrange("e a (q r) n -> r q (e a) n", r=4)
        for r in range(4):
            nc.sync.dma_start(ws[r:P:32, :, :].bitcast(I32), scale_rows[r])
        word_rows = w_words.bitcast(I32).rearrange("e a p n -> p (e a) n")
        for h in range(2):
            nc.sync.dma_start(ww[:, 8 * h : 8 * h + 8, :].bitcast(I32), word_rows[:, 8 * h : 8 * h + 8, :])

        def interleave(copy, a, c, lo, hi):
            copy(
                out=grouped[a][c][:, lo:hi, :].rearrange("p (g i) j -> p g j i", i=4),
                in_=raw[a][c][:, :, lo:hi].rearrange("p j (g i) -> p g j i", i=4),
            )

        def quantize(a, c):
            cols = slice(512 * c, 512 * (c + 1))
            nc.vector.quantize_mx(
                out=words[a][:, cols].bitcast(FP8X4),
                scales=scales[4 * a : P, cols],
                in_=grouped[a][c][:].rearrange("p w j -> p (w j)"),
            )

        def gather_words(a, lo, hi):
            nc.vector.tensor_copy(slot_words[a][:, lo:hi], words[a][:].indirect(offsets[:, lo // 16 : hi // 16]))

        def gather_scales(lo, hi):
            nc.vector.tensor_copy(slot_scales[0][:, lo:hi], scales[:].indirect(offsets[:, lo // 16 : hi // 16]))

        def move_scales(queue, lo, hi):
            queue.dma_start(slot_scales[1][: P - 4, lo:hi].bitcast(I32), slot_scales[0][4:P, lo:hi].bitcast(I32))

        def multiply(e0, t):
            bank = psum.tile([P, 2, C], F32, name="bank")
            for i in range(2):
                e = e0 + i
                for h in range(2):
                    cols = slice(C * e + P * h, C * e + P * (h + 1))
                    for a in range(2):
                        nc.tensor.matmul_mx(
                            out=bank[:, i, P * h : P * (h + 1)],
                            lhsT=ww[:, 2 * e + a, 2 * P * t : 2 * P * (t + 1)].bitcast(FP4X4),
                            lhsT_scale=ws[:, 2 * e + a, P * t : P * (t + 1)],
                            rhs=slot_words[a][:, cols].bitcast(FP8X4),
                            rhs_scale=slot_scales[a][:, cols],
                            start=(a == 0),
                            stop=(a == 1),
                        )
            return bank

        def relu(engine, bank, e, t):
            sums = bank[:, e % 2, :].rearrange("p (m u) -> p m u", u=U)
            if engine == "s":
                nc.scalar.activation(results[t][:, :, e, :], sums, RELU, bias=bias[:, t, e : e + 1])
            else:
                nc.vector.tensor_scalar(results[t][:, :, e, :], sums, bias[:, t, e : e + 1], 0.0, ADD, MAX)

        def square(engine, g, t, ranks):
            v = results[t][:, ranks, 4 * g : 4 * g + 4, :].rearrange("p m e u -> p m (e u)")
            if engine == "s":
                nc.scalar.activation(v, v, SQUARE)
            else:
                nc.vector.tensor_tensor(v, v, v, MULT)

        def store(t, ranks, lo, hi):
            rows = out[P * t : P * (t + 1), :].rearrange("p (m e u) -> p m e u", m=R, e=E)
            nc.sync.dma_start(rows[:, ranks, lo:hi, :], results[t][:, ranks, lo:hi, :])

        for c in range(2):
            interleave(nc.vector.tensor_copy, 0, c, 0, 384)
            interleave(nc.scalar.copy, 0, c, 384, 512)
            quantize(0, c)
        interleave(nc.scalar.copy, 1, 0, 0, 512)
        interleave(nc.scalar.copy, 1, 1, 128, 512)
        interleave(nc.vector.tensor_copy, 1, 1, 0, 128)
        gather_words(0, 0, 512)
        gather_words(0, 512, 1024)
        quantize(1, 0)
        quantize(1, 1)
        gather_scales(0, 512)
        move_scales(nc.scalar, 0, 512)
        gather_scales(512, 1024)
        move_scales(nc.scalar, 512, 1024)
        warm = psum.tile([P, 2, C], F32, name="bank")
        for i in range(12):
            nc.tensor.matmul_mx(
                out=warm[:, 0, :P],
                lhsT=ww[:, 0, : 2 * P].bitcast(FP4X4),
                lhsT_scale=ws[:, 0, :P],
                rhs=slot_words[0][:, :P].bitcast(FP8X4),
                rhs_scale=slot_scales[0][:, :P],
                start=True,
                stop=True,
            )
        gather_words(1, 0, 512)
        gather_words(1, 512, 1024)
        gather_words(0, 1024, 1536)
        gather_words(0, 1536, 2048)
        gather_scales(1024, 1536)
        move_scales(nc.sync, 1024, 1536)
        gather_scales(1536, 2048)
        move_scales(nc.sync, 1536, 2048)
        gather_words(1, 1024, 1536)
        gather_words(1, 1536, 2048)
        all_ranks = slice(0, R)
        halves = (slice(0, R // 2), slice(R // 2, R))
        for t in range(4):
            for e in (0, 2):
                bank = multiply(e, t)
                engine = "s" if e == 0 or t < 2 else "v"
                relu(engine, bank, e, t)
                relu(engine, bank, e + 1, t)
            for ranks in halves if t == 0 else (all_ranks,):
                square("s" if t < 2 else "v", 0, t, ranks)
                if t < 3:
                    store(t, ranks, 0, 4)
        for t in (3, 0, 1, 2):
            for e, engine in ((4, "v"), (6, "s")):
                bank = multiply(e, t)
                relu(engine, bank, e, t)
                relu(engine, bank, e + 1, t)
            for engine, ranks in zip("sv", halves):
                square(engine, 1, t, ranks)
                store(t, ranks, 0 if t == 3 else 4, 8)
